import numpy as np
import ml_dtypes


def mxq(x, axis, fmt="e4m3"):
    dtype, down = {"e4m3": (ml_dtypes.float8_e4m3fn, 7), "e5m2": (ml_dtypes.float8_e5m2, 14)}[fmt]
    v = np.moveaxis(np.asarray(x, np.float32).astype(ml_dtypes.bfloat16).astype(np.float64), axis, -1)
    blocks = v.reshape(v.shape[:-1] + (-1, 32))
    amax = np.abs(blocks).max(-1, keepdims=True)
    byte = np.maximum(np.where(amax > 0, np.frexp(amax)[1] - 1 + 127, 0) - down, 1)
    scale = np.exp2(byte - 127.0)
    codes = (blocks / scale).astype(np.float32).astype(dtype).astype(np.float64)
    return np.moveaxis((codes * scale).reshape(v.shape), -1, axis)


WIDE = False


def mx_kscale(k):
    if not WIDE:
        return np.ones(k)
    levels = np.array([10, -10, 5, -5, 0])
    if k % 512:
        return np.exp2(np.random.permutation(np.resize(levels, k // 32))).repeat(32)
    a = np.empty((k // 512, 16))
    for p in range(k // 512):
        a[p, :8] = np.random.permutation(np.resize(levels, 8))
        for g in range(8):
            far = levels[np.abs(levels - a[p, g]) >= 10]
            a[p, g + 8] = far[np.random.randint(len(far))]
    return np.exp2(a.ravel()).repeat(32)


def f64(x):
    return np.asarray(x).astype(np.float64)


def striped8(idx):
    return np.asarray(idx).reshape(8, -1, 16).transpose(0, 2, 1).reshape(128, -1).astype(np.uint16)


def unstriped8(offs):
    return offs.reshape(8, 16, -1).transpose(0, 2, 1).reshape(8, -1).astype(np.int64)


def pick8(x, idx, run):
    r = np.arange(len(x))
    return x[r[:, None], idx[r % (8 * run) // run]]


E2M1 = np.array([0.0, 0.5, 1.0, 1.5, 2.0, 3.0, 4.0, 6.0, -0.0, -0.5, -1.0, -1.5, -2.0, -3.0, -4.0, -6.0])


def pack_weight(w, fmt):
    k, n = w.shape
    w = f64(np.asarray(w, np.float32).astype(ml_dtypes.bfloat16)).reshape(k // 32, 32, n)
    amax = np.abs(w).max(1)
    if fmt == "e4m3":
        byte = np.frexp(amax)[1] - 1 + 127 - 7
    else:
        mant, ex = np.frexp(amax / 6.0)
        byte = np.where(mant > 0.5, ex, ex - 1) + 127
    byte = np.clip(np.where(amax > 0, byte, 1), 1, 254)
    scaled = (w * np.exp2(127.0 - byte)[:, None, :]).reshape(k, n).astype(np.float32)
    by_word = np.ascontiguousarray(scaled.reshape(k // 512, 128, 4, n).transpose(0, 1, 3, 2))
    if fmt == "e4m3":
        words = by_word.astype(ml_dtypes.float8_e4m3fn).view(np.uint8)
    else:
        c = by_word.astype(ml_dtypes.float4_e2m1fn).view(np.uint8) & 0xF
        words = (c[..., 0::2] | (c[..., 1::2] << 4)).reshape(k // 512, 128, 2 * n)
    return np.ascontiguousarray(words), np.ascontiguousarray(byte.astype(np.uint8).reshape(k // 512, 16, n))


def unpack_weight(words, scales, fmt):
    g, _, n = scales.shape
    words = np.ascontiguousarray(words).reshape(g, 128, n, -1)
    if fmt == "e4m3":
        vals = words.view(ml_dtypes.float8_e4m3fn).astype(np.float64)
    else:
        nib = np.empty((g, 128, n, 4), np.uint8)
        nib[..., 0::2] = words & 0xF
        nib[..., 1::2] = words >> 4
        vals = E2M1[nib]
    vals = vals * np.repeat(np.exp2(scales.astype(np.float64) - 127.0), 8, axis=1)[..., None]
    return vals.transpose(0, 1, 3, 2).reshape(g * 512, n)


D, E, T, Q, I, G = 512, 512, 1024, 128, 512, 64


def setup_inputs():
    n = np.random.standard_normal
    idx = np.stack([np.random.permutation(T)[:I] for _ in range(8)])
    fd = mx_kscale(D)
    fe = mx_kscale(E)
    keysp = pack_weight(n((D, T)) / fd[:, None], "e4m3")
    return {
        "query": (n((D, Q)) * 0.7 / np.sqrt(D) * fd[:, None]).astype(np.float32),
        "keys_words": keysp[0],
        "keys_scales": keysp[1],
        "gout": (n((E, Q)) * 1 / np.sqrt(E) * fe[:, None]).astype(np.float32),
        "vals": (n((E, T)) / fe[:, None]).astype(np.float32),
        "quota": (np.random.uniform(0.3, 2.0, (Q, G))).astype(np.float32),
        "old": (0.5 * n((Q, T))).astype(np.float32),
        "offs": striped8(idx),
    }


def reference(query, keys_words, keys_scales, gout, vals, quota, old, offs):
    idx = unstriped8(offs)
    keysu = unpack_weight(keys_words, keys_scales, "e4m3")
    queryq = mxq(f64(query), 0, "e4m3")
    a = queryq.T @ keysu
    p = np.exp(pick8(a, idx, 16))
    u1 = f64(quota) / p.reshape(Q, G, I // G).sum(axis=2)
    ur = np.repeat(u1, I // G, axis=1)
    goutq = mxq(f64(gout), 0, "e4m3")
    valsq = mxq(f64(vals), 0, "e4m3")
    c0 = goutq.T @ valsq
    dw = pick8(c0, idx, 16)
    dur = dw * p
    du1 = dur.reshape(Q, G, I // G).sum(axis=2)
    e1 = du1 * f64(quota) / np.square(p.reshape(Q, G, I // G).sum(axis=2)) * (-1.0)
    r1 = np.repeat(e1, I // G, axis=1)
    dp = dw * ur + r1
    e2 = dp * p
    s2 = np.zeros((Q, T))
    s2[np.arange(Q)[:, None], idx[np.arange(Q) % 128 // 16]] = e2
    y = s2 * 8.0 + f64(old)
    return y

@@ -1,0 +1,216 @@
+from contextlib import ExitStack
+
+import concourse.mybir as mybir
+
+F32 = mybir.dt.float32
+BF16 = mybir.dt.bfloat16
+I32 = mybir.dt.int32
+U32 = mybir.dt.uint32
+U16 = mybir.dt.uint16
+U8 = mybir.dt.uint8
+FP8X4 = mybir.dt.float8_e4m3fn_x4
+ALU = mybir.AluOpType
+ACT = mybir.ActivationFunctionType
+AX = mybir.AxisListType
+
+P = 128
+T, Q, SLOTS, G, GS = 1024, 128, 512, 64, 8
+FLOPS = 2 * 2 * 512 * Q * T
+
+VAL_LOADS = [[0,256],[256,256],[512,256],[768,256]]
+VAL_PIECES = [[0,256,0,"s"],[256,256,0,"s"],[512,256,256,"s"],[768,128,128,"s"],[896,128,0,"s"]]
+PARTS = 2
+TPARTS = 2
+
+
+def interleave(nc, eng, dst, src):
+    d = dst.rearrange("p (c i) t -> p c t i", i=4)
+    s = src.rearrange("p t (c i) -> p c t i", i=4)
+    if eng == "v":
+        nc.vector.tensor_copy(out=d, in_=s)
+    else:
+        nc.scalar.copy(out=dst, in_=src.rearrange("p t c -> p c t"))
+
+
+def copy_out(nc, eng, dst, src):
+    if eng == "v":
+        nc.vector.tensor_copy(out=dst, in_=src)
+    else:
+        nc.scalar.copy(out=dst, in_=src)
+
+
+def tile_attend_bquota_heads_kernel(tc, query, keys_words, keys_scales, gout, vals, quota, old, offs, out):
+    nc = tc.nc
+    with ExitStack() as ctx:
+        sb = ctx.enter_context(tc.tile_pool(name="sb", bufs=1))
+        ps = ctx.enter_context(tc.psum_pool(name="ps", bufs=1))
+
+        k_scales = sb.tile([P, T], U8, name="k_scales", align_bytes=64)
+        def load_scales(eng, quad):
+            eng.dma_start(
+                out=k_scales[32 * quad : 32 * quad + 4, :].bitcast(I32),
+                in_=keys_scales[0, 4 * quad : 4 * quad + 4, :].bitcast(I32),
+            )
+
+        load_scales(nc.scalar, 0)
+        load_scales(nc.scalar, 1)
+        warm = sb.tile([P, 8], F32, name="warm")
+        warm_out = sb.tile([P, 8], F32, name="warm_out")
+        nc.vector.memset(warm[:], 0.0)
+        nc.scalar.activation(out=warm_out[:], in_=warm[:], func=ACT.Exp)
+
+        q_raw = sb.tile([P, 4, Q], F32, name="q_raw")
+        nc.sync.dma_start(out=q_raw[:], in_=query.rearrange("(p j) c -> p j c", j=4))
+        load_scales(nc.sync, 2)
+        load_scales(nc.sync, 3)
+        k_flat = keys_words[0].rearrange("p n t -> p (n t)")
+        k_words = []
+        KW = T // 2
+        for h in range(2):
+            kw = sb.tile([P, KW], U32, name="k_words%d" % h, align_bytes=64)
+            nc.sync.dma_start(out=kw[:].bitcast(I32), in_=k_flat[:, 4 * KW * h : 4 * KW * (h + 1)].bitcast(I32))
+            k_words.append(kw)
+        g_raw = sb.tile([P, 4, Q], F32, name="g_raw")
+        nc.sync.dma_start(out=g_raw[:], in_=gout.rearrange("(p j) c -> p j c", j=4))
+        offsets = sb.tile([P, SLOTS // 16], U16, name="offsets")
+
+        vals_v = vals.rearrange("(p j) c -> p j c", j=4)
+        v_raw = []
+        for n, (c0, w) in enumerate(VAL_LOADS):
+            vr = sb.tile([P, 4, w], F32, name="v_raw%d" % n)
+            nc.sync.dma_start(out=vr[:], in_=vals_v[:, :, c0 : c0 + w])
+            v_raw.append(vr)
+            if n == 0:
+                nc.sync.dma_start(offsets[:], offs)
+        quota_sb = sb.tile([P, G], F32, name="quota_sb")
+        nc.sync.dma_start(out=quota_sb[:], in_=quota)
+        old_sb = sb.tile([P, T], F32, name="old_sb")
+        nc.sync.dma_start(out=old_sb[:], in_=old)
+
+        s2 = sb.tile([P, T], F32, name="s2")
+        nc.gpsimd.memset(s2[:], 0.0)
+
+        def quantize(name, bf, width):
+            codes = sb.tile([P, width], U32, name=name + "_codes", align_bytes=64)
+            scales = sb.tile([P, width], U8, name=name + "_scales", align_bytes=64)
+            nc.vector.quantize_mx(out=codes[:].bitcast(FP8X4), scales=scales[:], in_=bf[:].rearrange("p c t -> p (c t)"))
+            return codes, scales
+
+        q_bf = sb.tile([P, Q, 4], BF16, name="q_bf", align_bytes=64)
+        interleave(nc, "v", q_bf[:], q_raw[:])
+        q_codes, q_scales = quantize("q", q_bf, Q)
+        g_bf = sb.tile([P, Q, 4], BF16, name="g_bf", align_bytes=64)
+        interleave(nc, "v", g_bf[:], g_raw[:])
+        g_codes, g_scales = quantize("g", g_bf, Q)
+
+        a_sb = sb.tile([P, T], F32, name="a_sb")
+        for n in range(4):
+            bank = ps.tile([P, 256], F32, name="a_ps%d" % n, tag="bank%d" % n)
+            cols = slice(256 * n, 256 * (n + 1))
+            k0 = 256 * n % KW
+            nc.tensor.matmul_mx(out=bank[:], lhsT=q_codes[:].bitcast(FP8X4), lhsT_scale=q_scales[:],
+                                rhs=k_words[256 * n // KW][:, k0 : k0 + 256].bitcast(FP8X4), rhs_scale=k_scales[:, cols],
+                                start=True, stop=True)
+            copy_out(nc, "sssv"[n], a_sb[:, cols], bank[:])
+
+        def grouped(t, lo, hi):
+            return t[:, lo:hi].rearrange("p (g j) -> p g j", j=GS)
+
+        def spread(t, lo, hi):
+            return t[:, lo // GS : hi // GS].unsqueeze(2).to_broadcast([P, (hi - lo) // GS, GS])
+
+        a_slot = sb.tile([P, SLOTS], F32, name="a_slot")
+        a_max = sb.tile([P, G], F32, name="a_max")
+        a_rel = sb.tile([P, SLOTS], F32, name="a_rel")
+        p_slot = sb.tile([P, SLOTS], F32, name="p_slot")
+        spans = [(SLOTS // PARTS * n, SLOTS // PARTS * (n + 1)) for n in range(PARTS)]
+        for lo, hi in spans:
+            nc.vector.tensor_copy(out=a_slot[:, lo:hi], in_=a_sb[:].indirect(offsets[:, lo // 16 : hi // 16]))
+        for lo, hi in spans:
+            nc.vector.tensor_reduce(out=a_max[:, lo // GS : hi // GS], in_=grouped(a_slot, lo, hi), axis=AX.X, op=ALU.max)
+        for lo, hi in spans:
+            nc.vector.tensor_tensor(out=grouped(a_rel, lo, hi), in0=grouped(a_slot, lo, hi), in1=spread(a_max, lo, hi), op=ALU.subtract)
+
+        p_inv = sb.tile([P, G], F32, name="p_inv")
+        share = sb.tile([P, G], F32, name="share")
+        share_slot = sb.tile([P, SLOTS], F32, name="share_slot")
+
+        v_bf = []
+        def cast(n):
+            c0, w, cut, oeng = VAL_PIECES[n]
+            ld = [m for m, (l0, lw) in enumerate(VAL_LOADS) if l0 <= c0 < l0 + lw][0]
+            l0 = VAL_LOADS[ld][0]
+            bf = sb.tile([P, w, 4], BF16, name="v_bf%d" % n, tag="v_bf%d" % n, align_bytes=64)
+            if cut > 0:
+                interleave(nc, "v", bf[:, 0:cut, :], v_raw[ld][:, :, c0 - l0 : c0 - l0 + cut])
+            if cut < w:
+                interleave(nc, "s", bf[:, cut:w, :], v_raw[ld][:, :, c0 - l0 + cut : c0 - l0 + w])
+            v_bf.append(bf)
+
+        c_sb = sb.tile([P, T], F32, name="c_sb")
+        banks = []
+        def product(n):
+            c0, w, cut, oeng = VAL_PIECES[n]
+            v_codes, v_scales = quantize("v%d" % n, v_bf[n], w)
+            bank = ps.tile([P, w], F32, name="c_ps%d" % n, tag="bank%d" % ((n + 4) % 8))
+            nc.tensor.matmul_mx(out=bank[:], lhsT=g_codes[:].bitcast(FP8X4), lhsT_scale=g_scales[:],
+                                rhs=v_codes[:].bitcast(FP8X4), rhs_scale=v_scales[:], start=True, stop=True)
+            banks.append(bank)
+
+        def empty(n):
+            c0, w, cut, oeng = VAL_PIECES[n]
+            copy_out(nc, oeng, c_sb[:, c0 : c0 + w], banks[n][:])
+
+        def exps():
+            for lo, hi in spans:
+                nc.scalar.activation(out=p_slot[:, lo:hi], in_=a_rel[:, lo:hi], func=ACT.Exp)
+
+        def sums():
+            p_sum = sb.tile([P, G], F32, name="p_sum", tag="v_bf%d" % (len(VAL_PIECES) - 1), align_bytes=64)
+            nc.vector.tensor_reduce(out=p_sum[:], in_=grouped(p_slot, 0, SLOTS), axis=AX.X, op=ALU.add)
+            nc.vector.reciprocal(out=p_inv[:], in_=p_sum[:])
+            nc.vector.scalar_tensor_tensor(out=share[:], in0=p_inv[:], scalar=8.0, in1=quota_sb[:], op0=ALU.mult, op1=ALU.mult)
+
+        cast(0)
+        cast(1)
+        exps()
+        product(0)
+        cast(2)
+        product(1)
+        cast(3)
+        cast(4)
+        product(2)
+        product(3)
+        product(4)
+        empty(0)
+        empty(1)
+        empty(2)
+        empty(3)
+        empty(4)
+        sums()
+        nc.scalar.copy(out=grouped(share_slot, 0, SLOTS), in_=spread(share, 0, SLOTS))
+
+        dur = sb.tile([P, SLOTS], F32, name="dur")
+        du = sb.tile([P, G], F32, name="du")
+        mean = sb.tile([P, G], F32, name="mean")
+        p_mean = sb.tile([P, SLOTS], F32, name="p_mean")
+        centred = sb.tile([P, SLOTS], F32, name="centred")
+        spans = [(SLOTS // TPARTS * n, SLOTS // TPARTS * (n + 1)) for n in range(TPARTS)]
+        for lo, hi in spans:
+            nc.vector.tensor_tensor(out=dur[:, lo:hi], in0=c_sb[:].indirect(offsets[:, lo // 16 : hi // 16]), in1=p_slot[:, lo:hi], op=ALU.mult)
+        for lo, hi in spans:
+            nc.vector.tensor_reduce(out=du[:, lo // GS : hi // GS], in_=grouped(dur, lo, hi), axis=AX.X, op=ALU.add)
+        for lo, hi in spans:
+            nc.vector.tensor_tensor(out=mean[:, lo // GS : hi // GS], in0=du[:, lo // GS : hi // GS], in1=p_inv[:, lo // GS : hi // GS], op=ALU.mult)
+        for lo, hi in spans:
+            nc.vector.tensor_tensor(out=grouped(p_mean, lo, hi), in0=grouped(p_slot, lo, hi), in1=spread(mean, lo, hi), op=ALU.mult)
+        for lo, hi in spans:
+            nc.vector.tensor_tensor(out=centred[:, lo:hi], in0=dur[:, lo:hi], in1=p_mean[:, lo:hi], op=ALU.subtract)
+        nc.vector.tensor_tensor(out=s2[:].indirect(offsets[:]), in0=centred[:], in1=share_slot[:], op=ALU.mult)
+
+        for n, (c0, w) in enumerate([[0,320],[320,320],[640,256],[896,128]]):
+            cols = slice(c0, c0 + w)
+            res = sb.tile([P, w], F32, name="res%d" % n)
+            nc.vector.tensor_tensor(out=res[:], in0=s2[:, cols], in1=old_sb[:, cols], op=ALU.add)
+            eng = nc.sync if n % 2 == 0 else nc.scalar
+            eng.dma_start(out=out[:, cols], in_=res[:])

@@ -18,7 +18,8 @@ T, Q, SLOTS, G, GS = 1024, 128, 512, 64, 8
 FLOPS = 2 * 2 * 512 * Q * T
 
 VAL_LOADS = [[0,256],[256,256],[512,256],[768,256]]
-VAL_PIECES = [[0,256,0,"s"],[256,256,0,"s"],[512,256,256,"s"],[768,128,128,"s"],[896,128,0,"s"]]
+VAL_PIECES = [[0,256,[["v",256]],"s"],[256,256,[["s",256]],"s"],[512,256,[["s",256]],"s"],[768,128,[["v",128]],"s"],[896,128,[["v",128]],"s"]]
+A_PIECES = [[0,256,"s"],[256,256,"s"],[512,256,"s"],[768,256,"s"]]
 PARTS = 2
 TPARTS = 2
 
@@ -28,8 +29,10 @@ def interleave(nc, eng, dst, src):
     s = src.rearrange("p t (c i) -> p c t i", i=4)
     if eng == "v":
         nc.vector.tensor_copy(out=d, in_=s)
+    elif eng == "s":
+        nc.scalar.copy(out=d, in_=s)
     else:
-        nc.scalar.copy(out=dst, in_=src.rearrange("p t c -> p c t"))
+        nc.gpsimd.tensor_scalar(out=dst, in0=src.rearrange("p t c -> p c t"), scalar1=1.0, scalar2=0.0, op0=ALU.mult, op1=ALU.add)
 
 
 def copy_out(nc, eng, dst, src):
@@ -46,6 +49,7 @@ def tile_attend_bquota_heads_kernel(tc, query, keys_words, keys_scales, gout, va
         ps = ctx.enter_context(tc.psum_pool(name="ps", bufs=1))
 
         k_scales = sb.tile([P, T], U8, name="k_scales", align_bytes=64)
+
         def load_scales(eng, quad):
             eng.dma_start(
                 out=k_scales[32 * quad : 32 * quad + 4, :].bitcast(I32),
@@ -71,20 +75,31 @@ def tile_attend_bquota_heads_kernel(tc, query, keys_words, keys_scales, gout, va
             nc.sync.dma_start(out=kw[:].bitcast(I32), in_=k_flat[:, 4 * KW * h : 4 * KW * (h + 1)].bitcast(I32))
             k_words.append(kw)
         g_raw = sb.tile([P, 4, Q], F32, name="g_raw")
-        nc.sync.dma_start(out=g_raw[:], in_=gout.rearrange("(p j) c -> p j c", j=4))
         offsets = sb.tile([P, SLOTS // 16], U16, name="offsets")
-
+        quota_sb = sb.tile([P, G], F32, name="quota_sb")
+        old_sb = sb.tile([P, T], F32, name="old_sb")
         vals_v = vals.rearrange("(p j) c -> p j c", j=4)
         v_raw = []
-        for n, (c0, w) in enumerate(VAL_LOADS):
-            vr = sb.tile([P, 4, w], F32, name="v_raw%d" % n)
+
+        def load_v(n):
+            c0, w = VAL_LOADS[n]
+            vr = sb.tile([P, 4, w], F32, name="v_raw%d" % n, tag="v_raw%d" % n)
             nc.sync.dma_start(out=vr[:], in_=vals_v[:, :, c0 : c0 + w])
             v_raw.append(vr)
-            if n == 0:
-                nc.sync.dma_start(offsets[:], offs)
-        quota_sb = sb.tile([P, G], F32, name="quota_sb")
+
+        def load_g():
+            nc.sync.dma_start(out=g_raw[:], in_=gout.rearrange("(p j) c -> p j c", j=4))
+
+        def load_offs():
+            nc.sync.dma_start(offsets[:], offs)
+
+        load_v(0)
+        load_offs()
+        load_g()
+        load_v(1)
+        load_v(2)
+        load_v(3)
         nc.sync.dma_start(out=quota_sb[:], in_=quota)
-        old_sb = sb.tile([P, T], F32, name="old_sb")
         nc.sync.dma_start(out=old_sb[:], in_=old)
 
         s2 = sb.tile([P, T], F32, name="s2")
@@ -99,19 +114,16 @@ def tile_attend_bquota_heads_kernel(tc, query, keys_words, keys_scales, gout, va
         q_bf = sb.tile([P, Q, 4], BF16, name="q_bf", align_bytes=64)
         interleave(nc, "v", q_bf[:], q_raw[:])
         q_codes, q_scales = quantize("q", q_bf, Q)
-        g_bf = sb.tile([P, Q, 4], BF16, name="g_bf", align_bytes=64)
-        interleave(nc, "v", g_bf[:], g_raw[:])
-        g_codes, g_scales = quantize("g", g_bf, Q)
 
         a_sb = sb.tile([P, T], F32, name="a_sb")
-        for n in range(4):
-            bank = ps.tile([P, 256], F32, name="a_ps%d" % n, tag="bank%d" % n)
-            cols = slice(256 * n, 256 * (n + 1))
-            k0 = 256 * n % KW
+        for n, (c0, w, eng) in enumerate(A_PIECES):
+            bank = ps.tile([P, w], F32, name="a_ps%d" % n, tag="bank%d" % n)
+            cols = slice(c0, c0 + w)
+            k0 = c0 % KW
             nc.tensor.matmul_mx(out=bank[:], lhsT=q_codes[:].bitcast(FP8X4), lhsT_scale=q_scales[:],
-                                rhs=k_words[256 * n // KW][:, k0 : k0 + 256].bitcast(FP8X4), rhs_scale=k_scales[:, cols],
+                                rhs=k_words[c0 // KW][:, k0 : k0 + w].bitcast(FP8X4), rhs_scale=k_scales[:, cols],
                                 start=True, stop=True)
-            copy_out(nc, "sssv"[n], a_sb[:, cols], bank[:])
+            copy_out(nc, eng, a_sb[:, cols], bank[:])
 
         def grouped(t, lo, hi):
             return t[:, lo:hi].rearrange("p (g j) -> p g j", j=GS)
@@ -121,73 +133,104 @@ def tile_attend_bquota_heads_kernel(tc, query, keys_words, keys_scales, gout, va
 
         a_slot = sb.tile([P, SLOTS], F32, name="a_slot")
         a_max = sb.tile([P, G], F32, name="a_max")
-        a_rel = sb.tile([P, SLOTS], F32, name="a_rel")
-        p_slot = sb.tile([P, SLOTS], F32, name="p_slot")
+        a_rel = sb.tile([P, SLOTS], F32, name="a_rel", tag="a_rel")
         spans = [(SLOTS // PARTS * n, SLOTS // PARTS * (n + 1)) for n in range(PARTS)]
-        for lo, hi in spans:
-            nc.vector.tensor_copy(out=a_slot[:, lo:hi], in_=a_sb[:].indirect(offsets[:, lo // 16 : hi // 16]))
-        for lo, hi in spans:
-            nc.vector.tensor_reduce(out=a_max[:, lo // GS : hi // GS], in_=grouped(a_slot, lo, hi), axis=AX.X, op=ALU.max)
-        for lo, hi in spans:
-            nc.vector.tensor_tensor(out=grouped(a_rel, lo, hi), in0=grouped(a_slot, lo, hi), in1=spread(a_max, lo, hi), op=ALU.subtract)
+        def a_path():
+            for lo, hi in spans:
+                nc.vector.tensor_copy(out=a_slot[:, lo:hi], in_=a_sb[:].indirect(offsets[:, lo // 16 : hi // 16]))
+            for lo, hi in spans:
+                nc.vector.tensor_reduce(out=a_max[:, lo // GS : hi // GS], in_=grouped(a_slot, lo, hi), axis=AX.X, op=ALU.max)
+            for lo, hi in spans:
+                nc.vector.tensor_tensor(out=grouped(a_rel, lo, hi), in0=grouped(a_slot, lo, hi), in1=spread(a_max, lo, hi), op=ALU.subtract)
 
         p_inv = sb.tile([P, G], F32, name="p_inv")
         share = sb.tile([P, G], F32, name="share")
         share_slot = sb.tile([P, SLOTS], F32, name="share_slot")
 
-        v_bf = []
-        def cast(n):
-            c0, w, cut, oeng = VAL_PIECES[n]
+        v_bf = {}
+
+        def cast(n, part):
+            c0, w, cuts, oeng = VAL_PIECES[n]
             ld = [m for m, (l0, lw) in enumerate(VAL_LOADS) if l0 <= c0 < l0 + lw][0]
             l0 = VAL_LOADS[ld][0]
-            bf = sb.tile([P, w, 4], BF16, name="v_bf%d" % n, tag="v_bf%d" % n, align_bytes=64)
-            if cut > 0:
-                interleave(nc, "v", bf[:, 0:cut, :], v_raw[ld][:, :, c0 - l0 : c0 - l0 + cut])
-            if cut < w:
-                interleave(nc, "s", bf[:, cut:w, :], v_raw[ld][:, :, c0 - l0 + cut : c0 - l0 + w])
-            v_bf.append(bf)
+            if n not in v_bf:
+                v_bf[n] = sb.tile([P, w, 4], BF16, name="v_bf%d" % n, tag="v_bf%d" % n, align_bytes=64)
+            lo = sum(c for e, c in cuts[:part])
+            eng, cnt = cuts[part]
+            interleave(nc, eng, v_bf[n][:, lo : lo + cnt, :], v_raw[ld][:, :, c0 - l0 + lo : c0 - l0 + lo + cnt])
 
-        c_sb = sb.tile([P, T], F32, name="c_sb")
-        banks = []
+        g_bf = sb.tile([P, Q, 4], BF16, name="g_bf", align_bytes=64)
+        gq = []
+        vq = {}
+        banks = {}
+
+        def g_cast():
+            interleave(nc, "s", g_bf[:], g_raw[:])
+
+        def g_quant():
+            gq.extend(quantize("g", g_bf, Q))
+
+        v01_codes = sb.tile([P, 512], U32, name="v01_codes", align_bytes=64)
+        v01_scales = sb.tile([P, 512], U8, name="v01_scales", align_bytes=64)
+
+        def quant(n):
+            if n < 2:
+                cols = slice(256 * n, 256 * (n + 1))
+                nc.vector.quantize_mx(out=v01_codes[:, cols].bitcast(FP8X4), scales=v01_scales[:, cols], in_=v_bf[n][:].rearrange("p c t -> p (c t)"))
+                vq[1] = (v01_codes, v01_scales)
+            else:
+                vq[n] = quantize("v%d" % n, v_bf[n], VAL_PIECES[n][1])
+
         def product(n):
-            c0, w, cut, oeng = VAL_PIECES[n]
-            v_codes, v_scales = quantize("v%d" % n, v_bf[n], w)
-            bank = ps.tile([P, w], F32, name="c_ps%d" % n, tag="bank%d" % ((n + 4) % 8))
-            nc.tensor.matmul_mx(out=bank[:], lhsT=g_codes[:].bitcast(FP8X4), lhsT_scale=g_scales[:],
-                                rhs=v_codes[:].bitcast(FP8X4), rhs_scale=v_scales[:], start=True, stop=True)
-            banks.append(bank)
+            w = 512 if n == 1 else VAL_PIECES[n][1]
+            bank = ps.tile([P, w], F32, name="c_ps%d" % n, tag="bank%d" % ((n + len(A_PIECES)) % 8))
+            nc.tensor.matmul_mx(out=bank[:], lhsT=gq[0][:].bitcast(FP8X4), lhsT_scale=gq[1][:],
+                                rhs=vq[n][0][:].bitcast(FP8X4), rhs_scale=vq[n][1][:], start=True, stop=True)
+            banks[n] = bank
 
         def empty(n):
-            c0, w, cut, oeng = VAL_PIECES[n]
+            c0, w, cuts, oeng = VAL_PIECES[n]
+            if n == 1:
+                c0, w = 0, 512
             copy_out(nc, oeng, c_sb[:, c0 : c0 + w], banks[n][:])
 
+        keep = {}
+
         def exps():
-            for lo, hi in spans:
-                nc.scalar.activation(out=p_slot[:, lo:hi], in_=a_rel[:, lo:hi], func=ACT.Exp)
+            keep["p"] = sb.tile([P, SLOTS], F32, name="p_slot", tag="v_raw2")
+            nc.scalar.activation(out=keep["p"][:], in_=a_rel[:], func=ACT.Exp)
 
         def sums():
             p_sum = sb.tile([P, G], F32, name="p_sum", tag="v_bf%d" % (len(VAL_PIECES) - 1), align_bytes=64)
-            nc.vector.tensor_reduce(out=p_sum[:], in_=grouped(p_slot, 0, SLOTS), axis=AX.X, op=ALU.add)
+            nc.vector.tensor_reduce(out=p_sum[:], in_=grouped(keep["p"], 0, SLOTS), axis=AX.X, op=ALU.add)
             nc.vector.reciprocal(out=p_inv[:], in_=p_sum[:])
             nc.vector.scalar_tensor_tensor(out=share[:], in0=p_inv[:], scalar=8.0, in1=quota_sb[:], op0=ALU.mult, op1=ALU.mult)
 
-        cast(0)
-        cast(1)
+        g_cast()
+        g_quant()
+        a_path()
+        cast(0, 0)
+        quant(0)
+        cast(1, 0)
+        cast(2, 0)
         exps()
-        product(0)
-        cast(2)
+        quant(1)
         product(1)
-        cast(3)
-        cast(4)
+        cast(3, 0)
+        cast(4, 0)
+        quant(2)
         product(2)
+        quant(3)
         product(3)
+        quant(4)
         product(4)
-        empty(0)
+        c_sb = sb.tile([P, T], F32, name="c_sb", tag="a_rel")
         empty(1)
         empty(2)
         empty(3)
         empty(4)
         sums()
+        p_slot = keep["p"]
         nc.scalar.copy(out=grouped(share_slot, 0, SLOTS), in_=spread(share, 0, SLOTS))
 
         dur = sb.tile([P, SLOTS], F32, name="dur")
@@ -195,16 +238,16 @@ def tile_attend_bquota_heads_kernel(tc, query, keys_words, keys_scales, gout, va
         mean = sb.tile([P, G], F32, name="mean")
         p_mean = sb.tile([P, SLOTS], F32, name="p_mean")
         centred = sb.tile([P, SLOTS], F32, name="centred")
-        spans = [(SLOTS // TPARTS * n, SLOTS // TPARTS * (n + 1)) for n in range(TPARTS)]
-        for lo, hi in spans:
+        tspans = [(SLOTS // TPARTS * n, SLOTS // TPARTS * (n + 1)) for n in range(TPARTS)]
+        for lo, hi in tspans:
             nc.vector.tensor_tensor(out=dur[:, lo:hi], in0=c_sb[:].indirect(offsets[:, lo // 16 : hi // 16]), in1=p_slot[:, lo:hi], op=ALU.mult)
-        for lo, hi in spans:
+        for lo, hi in tspans:
             nc.vector.tensor_reduce(out=du[:, lo // GS : hi // GS], in_=grouped(dur, lo, hi), axis=AX.X, op=ALU.add)
-        for lo, hi in spans:
+        for lo, hi in tspans:
             nc.vector.tensor_tensor(out=mean[:, lo // GS : hi // GS], in0=du[:, lo // GS : hi // GS], in1=p_inv[:, lo // GS : hi // GS], op=ALU.mult)
-        for lo, hi in spans:
+        for lo, hi in tspans:
             nc.vector.tensor_tensor(out=grouped(p_mean, lo, hi), in0=grouped(p_slot, lo, hi), in1=spread(mean, lo, hi), op=ALU.mult)
-        for lo, hi in spans:
+        for lo, hi in tspans:
             nc.vector.tensor_tensor(out=centred[:, lo:hi], in0=dur[:, lo:hi], in1=p_mean[:, lo:hi], op=ALU.subtract)
         nc.vector.tensor_tensor(out=s2[:].indirect(offsets[:]), in0=centred[:], in1=share_slot[:], op=ALU.mult)
 

from contextlib import ExitStack

import concourse.mybir as mybir

F32 = mybir.dt.float32
BF16 = mybir.dt.bfloat16
I32 = mybir.dt.int32
U32 = mybir.dt.uint32
U16 = mybir.dt.uint16
U8 = mybir.dt.uint8
FP8X4 = mybir.dt.float8_e4m3fn_x4
ALU = mybir.AluOpType
ACT = mybir.ActivationFunctionType
AX = mybir.AxisListType

P = 128
T, Q, SLOTS, G, GS = 1024, 128, 512, 64, 8
FLOPS = 2 * 2 * 512 * Q * T

VAL_LOADS = [[0,256],[256,256],[512,256],[768,256]]
VAL_PIECES = [[0,256,[["v",256]],"s"],[256,256,[["s",256]],"s"],[512,256,[["s",256]],"s"],[768,128,[["v",128]],"s"],[896,128,[["v",128]],"s"]]
A_PIECES = [[0,256,"s"],[256,256,"s"],[512,256,"s"],[768,256,"s"]]
PARTS = 2
TPARTS = 2


def interleave(nc, eng, dst, src):
    d = dst.rearrange("p (c i) t -> p c t i", i=4)
    s = src.rearrange("p t (c i) -> p c t i", i=4)
    if eng == "v":
        nc.vector.tensor_copy(out=d, in_=s)
    elif eng == "s":
        nc.scalar.copy(out=d, in_=s)
    else:
        nc.gpsimd.tensor_scalar(out=dst, in0=src.rearrange("p t c -> p c t"), scalar1=1.0, scalar2=0.0, op0=ALU.mult, op1=ALU.add)


def copy_out(nc, eng, dst, src):
    if eng == "v":
        nc.vector.tensor_copy(out=dst, in_=src)
    else:
        nc.scalar.copy(out=dst, in_=src)


def tile_attend_bquota_heads_kernel(tc, query, keys_words, keys_scales, gout, vals, quota, old, offs, out):
    nc = tc.nc
    with ExitStack() as ctx:
        sb = ctx.enter_context(tc.tile_pool(name="sb", bufs=1))
        ps = ctx.enter_context(tc.psum_pool(name="ps", bufs=1))

        k_scales = sb.tile([P, T], U8, name="k_scales", align_bytes=64)

        def load_scales(eng, quad):
            eng.dma_start(
                out=k_scales[32 * quad : 32 * quad + 4, :].bitcast(I32),
                in_=keys_scales[0, 4 * quad : 4 * quad + 4, :].bitcast(I32),
            )

        load_scales(nc.scalar, 0)
        load_scales(nc.scalar, 1)
        warm = sb.tile([P, 8], F32, name="warm")
        warm_out = sb.tile([P, 8], F32, name="warm_out")
        nc.vector.memset(warm[:], 0.0)
        nc.scalar.activation(out=warm_out[:], in_=warm[:], func=ACT.Exp)

        q_raw = sb.tile([P, 4, Q], F32, name="q_raw")
        nc.sync.dma_start(out=q_raw[:], in_=query.rearrange("(p j) c -> p j c", j=4))
        load_scales(nc.sync, 2)
        load_scales(nc.sync, 3)
        k_flat = keys_words[0].rearrange("p n t -> p (n t)")
        k_words = []
        KW = T // 2
        for h in range(2):
            kw = sb.tile([P, KW], U32, name="k_words%d" % h, align_bytes=64)
            nc.sync.dma_start(out=kw[:].bitcast(I32), in_=k_flat[:, 4 * KW * h : 4 * KW * (h + 1)].bitcast(I32))
            k_words.append(kw)
        g_raw = sb.tile([P, 4, Q], F32, name="g_raw")
        offsets = sb.tile([P, SLOTS // 16], U16, name="offsets")
        quota_sb = sb.tile([P, G], F32, name="quota_sb")
        old_sb = sb.tile([P, T], F32, name="old_sb")
        vals_v = vals.rearrange("(p j) c -> p j c", j=4)
        v_raw = []

        def load_v(n):
            c0, w = VAL_LOADS[n]
            vr = sb.tile([P, 4, w], F32, name="v_raw%d" % n, tag="v_raw%d" % n)
            nc.sync.dma_start(out=vr[:], in_=vals_v[:, :, c0 : c0 + w])
            v_raw.append(vr)

        def load_g():
            nc.sync.dma_start(out=g_raw[:], in_=gout.rearrange("(p j) c -> p j c", j=4))

        def load_offs():
            nc.sync.dma_start(offsets[:], offs)

        load_v(0)
        load_offs()
        load_g()
        load_v(1)
        load_v(2)
        load_v(3)
        nc.sync.dma_start(out=quota_sb[:], in_=quota)
        nc.sync.dma_start(out=old_sb[:], in_=old)

        s2 = sb.tile([P, T], F32, name="s2")
        nc.gpsimd.memset(s2[:], 0.0)

        def quantize(name, bf, width):
            codes = sb.tile([P, width], U32, name=name + "_codes", align_bytes=64)
            scales = sb.tile([P, width], U8, name=name + "_scales", align_bytes=64)
            nc.vector.quantize_mx(out=codes[:].bitcast(FP8X4), scales=scales[:], in_=bf[:].rearrange("p c t -> p (c t)"))
            return codes, scales

        q_bf = sb.tile([P, Q, 4], BF16, name="q_bf", align_bytes=64)
        interleave(nc, "v", q_bf[:], q_raw[:])
        q_codes, q_scales = quantize("q", q_bf, Q)

        a_sb = sb.tile([P, T], F32, name="a_sb")
        for n, (c0, w, eng) in enumerate(A_PIECES):
            bank = ps.tile([P, w], F32, name="a_ps%d" % n, tag="bank%d" % n)
            cols = slice(c0, c0 + w)
            k0 = c0 % KW
            nc.tensor.matmul_mx(out=bank[:], lhsT=q_codes[:].bitcast(FP8X4), lhsT_scale=q_scales[:],
                                rhs=k_words[c0 // KW][:, k0 : k0 + w].bitcast(FP8X4), rhs_scale=k_scales[:, cols],
                                start=True, stop=True)
            copy_out(nc, eng, a_sb[:, cols], bank[:])

        def grouped(t, lo, hi):
            return t[:, lo:hi].rearrange("p (g j) -> p g j", j=GS)

        def spread(t, lo, hi):
            return t[:, lo // GS : hi // GS].unsqueeze(2).to_broadcast([P, (hi - lo) // GS, GS])

        a_slot = sb.tile([P, SLOTS], F32, name="a_slot")
        a_max = sb.tile([P, G], F32, name="a_max")
        a_rel = sb.tile([P, SLOTS], F32, name="a_rel", tag="a_rel")
        spans = [(SLOTS // PARTS * n, SLOTS // PARTS * (n + 1)) for n in range(PARTS)]
        def a_path():
            for lo, hi in spans:
                nc.vector.tensor_copy(out=a_slot[:, lo:hi], in_=a_sb[:].indirect(offsets[:, lo // 16 : hi // 16]))
            for lo, hi in spans:
                nc.vector.tensor_reduce(out=a_max[:, lo // GS : hi // GS], in_=grouped(a_slot, lo, hi), axis=AX.X, op=ALU.max)
            for lo, hi in spans:
                nc.vector.tensor_tensor(out=grouped(a_rel, lo, hi), in0=grouped(a_slot, lo, hi), in1=spread(a_max, lo, hi), op=ALU.subtract)

        p_inv = sb.tile([P, G], F32, name="p_inv")
        share = sb.tile([P, G], F32, name="share")
        share_slot = sb.tile([P, SLOTS], F32, name="share_slot")

        v_bf = {}

        def cast(n, part):
            c0, w, cuts, oeng = VAL_PIECES[n]
            ld = [m for m, (l0, lw) in enumerate(VAL_LOADS) if l0 <= c0 < l0 + lw][0]
            l0 = VAL_LOADS[ld][0]
            if n not in v_bf:
                v_bf[n] = sb.tile([P, w, 4], BF16, name="v_bf%d" % n, tag="v_bf%d" % n, align_bytes=64)
            lo = sum(c for e, c in cuts[:part])
            eng, cnt = cuts[part]
            interleave(nc, eng, v_bf[n][:, lo : lo + cnt, :], v_raw[ld][:, :, c0 - l0 + lo : c0 - l0 + lo + cnt])

        g_bf = sb.tile([P, Q, 4], BF16, name="g_bf", align_bytes=64)
        gq = []
        vq = {}
        banks = {}

        def g_cast():
            interleave(nc, "s", g_bf[:], g_raw[:])

        def g_quant():
            gq.extend(quantize("g", g_bf, Q))

        v01_codes = sb.tile([P, 512], U32, name="v01_codes", align_bytes=64)
        v01_scales = sb.tile([P, 512], U8, name="v01_scales", align_bytes=64)

        def quant(n):
            if n < 2:
                cols = slice(256 * n, 256 * (n + 1))
                nc.vector.quantize_mx(out=v01_codes[:, cols].bitcast(FP8X4), scales=v01_scales[:, cols], in_=v_bf[n][:].rearrange("p c t -> p (c t)"))
                vq[1] = (v01_codes, v01_scales)
            else:
                vq[n] = quantize("v%d" % n, v_bf[n], VAL_PIECES[n][1])

        def product(n):
            w = 512 if n == 1 else VAL_PIECES[n][1]
            bank = ps.tile([P, w], F32, name="c_ps%d" % n, tag="bank%d" % ((n + len(A_PIECES)) % 8))
            nc.tensor.matmul_mx(out=bank[:], lhsT=gq[0][:].bitcast(FP8X4), lhsT_scale=gq[1][:],
                                rhs=vq[n][0][:].bitcast(FP8X4), rhs_scale=vq[n][1][:], start=True, stop=True)
            banks[n] = bank

        def empty(n):
            c0, w, cuts, oeng = VAL_PIECES[n]
            if n == 1:
                c0, w = 0, 512
            copy_out(nc, oeng, c_sb[:, c0 : c0 + w], banks[n][:])

        keep = {}

        def exps():
            keep["p"] = sb.tile([P, SLOTS], F32, name="p_slot", tag="v_raw2")
            nc.scalar.activation(out=keep["p"][:], in_=a_rel[:], func=ACT.Exp)

        def sums():
            p_sum = sb.tile([P, G], F32, name="p_sum", tag="v_bf%d" % (len(VAL_PIECES) - 1), align_bytes=64)
            nc.vector.tensor_reduce(out=p_sum[:], in_=grouped(keep["p"], 0, SLOTS), axis=AX.X, op=ALU.add)
            nc.vector.reciprocal(out=p_inv[:], in_=p_sum[:])
            nc.vector.scalar_tensor_tensor(out=share[:], in0=p_inv[:], scalar=8.0, in1=quota_sb[:], op0=ALU.mult, op1=ALU.mult)

        g_cast()
        g_quant()
        a_path()
        cast(0, 0)
        quant(0)
        cast(1, 0)
        cast(2, 0)
        exps()
        quant(1)
        product(1)
        cast(3, 0)
        cast(4, 0)
        quant(2)
        product(2)
        quant(3)
        product(3)
        quant(4)
        product(4)
        c_sb = sb.tile([P, T], F32, name="c_sb", tag="a_rel")
        empty(1)
        empty(2)
        empty(3)
        empty(4)
        sums()
        p_slot = keep["p"]
        nc.scalar.copy(out=grouped(share_slot, 0, SLOTS), in_=spread(share, 0, SLOTS))

        dur = sb.tile([P, SLOTS], F32, name="dur")
        du = sb.tile([P, G], F32, name="du")
        mean = sb.tile([P, G], F32, name="mean")
        p_mean = sb.tile([P, SLOTS], F32, name="p_mean")
        centred = sb.tile([P, SLOTS], F32, name="centred")
        tspans = [(SLOTS // TPARTS * n, SLOTS // TPARTS * (n + 1)) for n in range(TPARTS)]
        for lo, hi in tspans:
            nc.vector.tensor_tensor(out=dur[:, lo:hi], in0=c_sb[:].indirect(offsets[:, lo // 16 : hi // 16]), in1=p_slot[:, lo:hi], op=ALU.mult)
        for lo, hi in tspans:
            nc.vector.tensor_reduce(out=du[:, lo // GS : hi // GS], in_=grouped(dur, lo, hi), axis=AX.X, op=ALU.add)
        for lo, hi in tspans:
            nc.vector.tensor_tensor(out=mean[:, lo // GS : hi // GS], in0=du[:, lo // GS : hi // GS], in1=p_inv[:, lo // GS : hi // GS], op=ALU.mult)
        for lo, hi in tspans:
            nc.vector.tensor_tensor(out=grouped(p_mean, lo, hi), in0=grouped(p_slot, lo, hi), in1=spread(mean, lo, hi), op=ALU.mult)
        for lo, hi in tspans:
            nc.vector.tensor_tensor(out=centred[:, lo:hi], in0=dur[:, lo:hi], in1=p_mean[:, lo:hi], op=ALU.subtract)
        nc.vector.tensor_tensor(out=s2[:].indirect(offsets[:]), in0=centred[:], in1=share_slot[:], op=ALU.mult)

        for n, (c0, w) in enumerate([[0,320],[320,320],[640,256],[896,128]]):
            cols = slice(c0, c0 + w)
            res = sb.tile([P, w], F32, name="res%d" % n)
            nc.vector.tensor_tensor(out=res[:], in0=s2[:, cols], in1=old_sb[:, cols], op=ALU.add)
            eng = nc.sync if n % 2 == 0 else nc.scalar
            eng.dma_start(out=out[:, cols], in_=res[:])
